import numpy as np
import ml_dtypes


def mxq(x, axis, fmt="e4m3"):
    dtype, down = {"e4m3": (ml_dtypes.float8_e4m3fn, 7), "e5m2": (ml_dtypes.float8_e5m2, 14)}[fmt]
    v = np.moveaxis(np.asarray(x, np.float32).astype(ml_dtypes.bfloat16).astype(np.float64), axis, -1)
    blocks = v.reshape(v.shape[:-1] + (-1, 32))
    amax = np.abs(blocks).max(-1, keepdims=True)
    byte = np.maximum(np.where(amax > 0, np.frexp(amax)[1] - 1 + 127, 0) - down, 1)
    scale = np.exp2(byte - 127.0)
    codes = (blocks / scale).astype(np.float32).astype(dtype).astype(np.float64)
    return np.moveaxis((codes * scale).reshape(v.shape), -1, axis)


WIDE = False


def mx_kscale(k):
    if not WIDE:
        return np.ones(k)
    levels = np.array([10, -10, 5, -5, 0])
    if k % 512:
        return np.exp2(np.random.permutation(np.resize(levels, k // 32))).repeat(32)
    a = np.empty((k // 512, 16))
    for p in range(k // 512):
        a[p, :8] = np.random.permutation(np.resize(levels, 8))
        for g in range(8):
            far = levels[np.abs(levels - a[p, g]) >= 10]
            a[p, g + 8] = far[np.random.randint(len(far))]
    return np.exp2(a.ravel()).repeat(32)


BF16 = ml_dtypes.bfloat16


def bf(x):
    return np.asarray(x, np.float32).astype(BF16)


def f64(x):
    return np.asarray(x).astype(np.float64)


E2M1 = np.array([0.0, 0.5, 1.0, 1.5, 2.0, 3.0, 4.0, 6.0, -0.0, -0.5, -1.0, -1.5, -2.0, -3.0, -4.0, -6.0])


def pack_weight(w, fmt):
    k, n = w.shape
    w = f64(bf(w)).reshape(k // 32, 32, n)
    amax = np.abs(w).max(1)
    if fmt == "e4m3":
        byte = np.frexp(amax)[1] - 1 + 127 - 7
    else:
        mant, ex = np.frexp(amax / 6.0)
        byte = np.where(mant > 0.5, ex, ex - 1) + 127
    byte = np.clip(np.where(amax > 0, byte, 1), 1, 254)
    scaled = (w * np.exp2(127.0 - byte)[:, None, :]).reshape(k, n).astype(np.float32)
    by_word = np.ascontiguousarray(scaled.reshape(k // 512, 128, 4, n).transpose(0, 1, 3, 2))
    if fmt == "e4m3":
        words = by_word.astype(ml_dtypes.float8_e4m3fn).view(np.uint8)
    else:
        c = by_word.astype(ml_dtypes.float4_e2m1fn).view(np.uint8) & 0xF
        words = c[..., 0::2] | (c[..., 1::2] << 4)
    return np.ascontiguousarray(words), np.ascontiguousarray(byte.astype(np.uint8).reshape(k // 512, 16, n))


def unpack_weight(words, scales, fmt):
    g, p, n, _ = words.shape
    if fmt == "e4m3":
        vals = np.ascontiguousarray(words).view(ml_dtypes.float8_e4m3fn).astype(np.float64)
    else:
        nib = np.empty((g, p, n, 4), np.uint8)
        nib[..., 0::2] = words & 0xF
        nib[..., 1::2] = words >> 4
        vals = E2M1[nib]
    vals = vals * np.repeat(np.exp2(scales.astype(np.float64) - 127.0), 8, axis=1)[..., None]
    return vals.transpose(0, 1, 3, 2).reshape(g * 512, n)
def pack4(w):
    words, scales = pack_weight(w, "e2m1")
    return words.reshape(words.shape[0], 128, -1), scales


def unpack4(words, scales):
    return unpack_weight(words.reshape(words.shape[0], 128, -1, 2), scales, "e2m1")


F, P, G, D, C, J = 8, 512, 8, 64, 512, 512


def setup_inputs():
    a = mx_kscale(P)
    t = mx_kscale(G * J)
    u = mx_kscale(C)
    tf = t.reshape(G, F, D).transpose(1, 0, 2).reshape(F, C)
    u2 = np.tile(u.reshape(G, D), (1, F))
    w1 = np.random.standard_normal((P, P)) / (3 * np.sqrt(P)) / a[:, None]
    w2 = np.random.standard_normal((G, J, J)) / (3 * np.sqrt(J)) / t.reshape(G, J, 1) * u2[:, None, :]
    w3 = np.random.standard_normal((C, C)) / np.sqrt(C) / u[:, None]
    w1_words, w1_scales = pack4(w1)
    w2_words, w2_scales = pack4(w2.reshape(G * J, J))
    w3_words, w3_scales = pack4(w3)
    return {"x": bf(np.random.standard_normal((F, P, C)) * a[:, None] * tf[:, None, :]),
            "w1_words": w1_words, "w1_scales": w1_scales,
            "w2_words": w2_words, "w2_scales": w2_scales,
            "w3_words": w3_words, "w3_scales": w3_scales,
            "skip1": bf((1 + 0.1 * np.random.standard_normal(P)) / a),
            "skip2": bf((1 + 0.1 * np.random.standard_normal((F, C))) * u / tf),
            "speed": bf(np.abs(np.random.standard_normal((F, P))))}


def reference(x, w1_words, w1_scales, w2_words, w2_scales, w3_words, w3_scales, skip1, skip2, speed):
    x = f64(x)
    w1 = unpack4(w1_words, w1_scales)
    w2 = unpack4(w2_words, w2_scales).reshape(G, J, J)
    w3 = unpack4(w3_words, w3_scales)
    y = x * f64(skip1)[:, None] + (w1.T @ mxq(x, 1, "e4m3"))
    yb = y.reshape(F, P, G, D).transpose(2, 1, 0, 3).reshape(G, P, J)
    m = mxq(yb, 2, "e4m3") @ w2
    m = m.reshape(G, P, F, D).transpose(2, 1, 0, 3).reshape(F, P, C)
    z = y * f64(skip2)[:, None, :] + m
    return np.tanh(f64(speed))[:, :, None] * (mxq(z, 2, "e4m3") @ w3)

@@ -1,0 +1,336 @@
+from contextlib import ExitStack
+
+import concourse.mybir as mybir
+from concourse.masks import make_identity
+
+F32 = mybir.dt.float32
+BF16 = mybir.dt.bfloat16
+I32 = mybir.dt.int32
+U32 = mybir.dt.uint32
+U8 = mybir.dt.uint8
+E4M3 = mybir.dt.float8_e4m3fn_x4
+E2M1 = mybir.dt.float4_e2m1fn_x4
+ALU = mybir.AluOpType
+ACT = mybir.ActivationFunctionType
+
+P = 128
+FR = 8
+NB = 8
+C = 512
+FLOPS = 3 * 2 * 8 * 512 * 512 * 512
+
+
+def tile_video_token_mixer_t2_kernel(
+    tc, x, w1_words, w1_scales, w2_words, w2_scales, w3_words, w3_scales, skip1, skip2, speed, out
+):
+    nc = tc.nc
+    with ExitStack() as ctx:
+        keep = ctx.enter_context(tc.tile_pool(name="keep", bufs=1))
+        raws = ctx.enter_context(tc.tile_pool(name="raws", bufs=5))
+        work = ctx.enter_context(tc.tile_pool(name="work", bufs=2))
+        y2s = ctx.enter_context(tc.tile_pool(name="y2s", bufs=10))
+        outs = ctx.enter_context(tc.tile_pool(name="outs", bufs=6))
+        psv = ctx.enter_context(tc.psum_pool(name="psv", bufs=4))
+        pss = ctx.enter_context(tc.psum_pool(name="pss", bufs=4))
+
+        w1_raw = keep.tile([P, 1024], U8, name="w1_raw", align_bytes=64)
+        w1s_raw = keep.tile([P, 512], U8, name="w1s_raw", align_bytes=64)
+        w1 = keep.tile([P, 4, 256], U8, name="w1", align_bytes=64)
+        w1s = keep.tile([P, 4, 128], U8, name="w1s", align_bytes=64)
+        w2 = keep.tile([P, NB, 1024], U8, name="w2", align_bytes=64)
+        w2s = keep.tile([P, NB, 512], U8, name="w2s", align_bytes=64)
+        w3 = keep.tile([P, 1024], U8, name="w3", align_bytes=64)
+        w3s = keep.tile([P, 512], U8, name="w3s", align_bytes=64)
+        ident = keep.tile([P, P], F32, name="ident", align_bytes=64)
+        s1 = keep.tile([P, 4], BF16, name="s1")
+        s1f = keep.tile([P, 4], F32, name="s1f")
+        s2 = keep.tile([P, FR, C], BF16, name="s2", align_bytes=64)
+        sp = keep.tile([P, FR, 4], BF16, name="sp")
+        gate = keep.tile([P, FR, 4], F32, name="gate")
+        warm = keep.tile([P, 1], F32, name="warm")
+        xg = [keep.tile([P, C, 4], BF16, name=f"xg{f}", align_bytes=64) for f in range(FR)]
+        xc = [keep.tile([P, C], U32, name=f"xc{f}", align_bytes=64) for f in range(FR)]
+        xs = [keep.tile([P, C], U8, name=f"xs{f}", align_bytes=64) for f in range(FR)]
+
+        with tc.manual_schedule():
+            nc.vector.memset(w1s_raw[:].bitcast(I32), 0)
+            nc.vector.memset(warm[:], 0.0)
+            nc.vector.memset(w2s[:].rearrange("p b n -> p (b n)").bitcast(I32), 0)
+            nc.vector.memset(w3s[:].bitcast(I32), 0)
+            nc.scalar.activation(out=warm[:], in_=warm[:], func=ACT.Tanh)
+            nc.sync.dma_start(out=w1_raw[:].bitcast(I32), in_=w1_words[0].bitcast(I32))
+            xr = []
+            for f in range(FR):
+                t = raws.tile([P, 4, C], BF16, name="xraw", align_bytes=64)
+                nc.sync.dma_start(out=t[:], in_=x[f].rearrange("(p j) c -> p j c", j=4))
+                xr.append(t)
+            for q in range(4):
+                nc.gpsimd.dma_start(
+                    out=w1s_raw[32 * q : 32 * q + 4, :].bitcast(I32),
+                    in_=w1_scales[0, 4 * q : 4 * q + 4, :].bitcast(I32),
+                )
+            nc.gpsimd.dma_start(out=s1[:], in_=skip1.rearrange("(p j) -> p j", j=4))
+            nc.gpsimd.dma_start(out=sp[:], in_=speed.rearrange("f (p j) -> p f j", j=4))
+            make_identity(nc, ident[:])
+            nc.sync.dma_start(
+                out=s2[:].rearrange("p f c -> p (f c)"),
+                in_=skip2.rearrange("f c -> (f c)").partition_broadcast(P),
+            )
+            nc.sync.dma_start(
+                out=w2[:].bitcast(I32), in_=w2_words.rearrange("g p n -> p g n").bitcast(I32)
+            )
+            for q in range(4):
+                nc.gpsimd.dma_start(
+                    out=w2s[32 * q : 32 * q + 4, :, :].bitcast(I32),
+                    in_=w2_scales[:, 4 * q : 4 * q + 4, :].rearrange("g r n -> r g n").bitcast(I32),
+                )
+            nc.sync.dma_start(out=w3[:].bitcast(I32), in_=w3_words[0].bitcast(I32))
+            for q in range(4):
+                nc.gpsimd.dma_start(
+                    out=w3s[32 * q : 32 * q + 4, :].bitcast(I32),
+                    in_=w3_scales[0, 4 * q : 4 * q + 4, :].bitcast(I32),
+                )
+
+            nc.vector.tensor_copy(
+                out=w1s[:], in_=w1s_raw[:].rearrange("p (m j) -> p j m", j=4)
+            )
+            nc.vector.tensor_copy(
+                out=w1[:].rearrange("p j (m e) -> p j m e", e=2),
+                in_=w1_raw[:].rearrange("p (m j e) -> p j m e", j=4, e=2),
+            )
+            nc.vector.tensor_copy(out=s1f[:], in_=s1[:])
+
+            def interleave(f, eng, t0, t1):
+                dst = xg[f][:].rearrange("p (t a) j -> p t a j", t=4)[:, t0:t1]
+                src = xr[f][:].rearrange("p j (a t) -> p t a j", t=4)[:, t0:t1]
+                if t1 - t0 == 1:
+                    dst, src = dst[:, 0], src[:, 0]
+                if eng == "v":
+                    nc.vector.tensor_copy(out=dst, in_=src)
+                else:
+                    nc.scalar.copy(out=dst, in_=src)
+
+            def quant_x(f):
+                nc.vector.quantize_mx(
+                    out=xc[f][:].bitcast(E4M3),
+                    scales=xs[f][:],
+                    in_=xg[f][:].rearrange("p c j -> p (c j)"),
+                )
+
+            state = {}
+
+            def stage1_mm(k, f):
+                ps = psv.tile([P, C], F32, name="pv")
+                nc.tensor.matmul_mx(
+                    out=ps[:],
+                    lhsT=w1[:, k, :].bitcast(E2M1),
+                    lhsT_scale=w1s[:, k, :],
+                    rhs=xc[f][:].bitcast(E4M3),
+                    rhs_scale=xs[f][:],
+                    start=True,
+                    stop=True,
+                )
+                state[("p1", k, f)] = ps
+
+            def stage1_exit(k, f):
+                if f == 0:
+                    ytile = work.tile([P, 32, P], F32, name="y", align_bytes=64)
+                    state[("y", k)] = ytile
+                y = state[("y", k)]
+                nc.vector.scalar_tensor_tensor(
+                    out=y[:, :, 16 * f : 16 * f + 16],
+                    in0=xg[f][:, :, k].rearrange("p (a q) -> p a q", q=16),
+                    scalar=s1f[:, k : k + 1],
+                    in1=state[("p1", k, f)][:].rearrange("p (a q) -> p a q", q=16),
+                    op0=ALU.mult,
+                    op1=ALU.add,
+                )
+
+            def skip_y(k, b):
+                y2 = y2s.tile([P, C], F32, name="y2", align_bytes=64)
+                y = state[("y", k)]
+                nc.gpsimd.tensor_tensor(
+                    out=y2[:].rearrange("p (f q t) -> p f q t", f=FR, t=4),
+                    in0=y[:].rearrange("p (t b) (f q) -> p b f q t", t=4, q=16)[:, b],
+                    in1=s2[:, :, 64 * b : 64 * b + 64].rearrange("p f (q t) -> p f q t", t=4),
+                    op=ALU.mult,
+                )
+                state[("y2", k, b)] = y2
+
+            def y_turn(k, b):
+                y = state[("y", k)]
+                ps = pss.tile([P, 4, P], F32, name="pt")
+                for t in range(4):
+                    nc.tensor.transpose(ps[:, t, :], y[:, 8 * t + b, :], ident[:])
+                state[("pt", k, b)] = ps
+
+            def y_turn_exit(k, b):
+                if b == 0:
+                    ytile = work.tile([P, NB, P, 4], BF16, name="yT", align_bytes=64)
+                    state[("yT", k)] = ytile
+                nc.scalar.copy(
+                    out=state[("yT", k)][:, b],
+                    in_=state[("pt", k, b)][:].rearrange("p t n -> p n t"),
+                )
+
+            def quant_y(k, h):
+                if h == 0:
+                    yc = work.tile([P, NB * P], U32, name="yc", align_bytes=64)
+                    ys = work.tile([P, NB * P], U8, name="ys", align_bytes=64)
+                    state[("yc", k)] = (yc, ys)
+                yc, ys = state[("yc", k)]
+                nc.vector.quantize_mx(
+                    out=yc[:, 512 * h : 512 * h + 512].bitcast(E4M3),
+                    scales=ys[:, 512 * h : 512 * h + 512],
+                    in_=state[("yT", k)][:, 4 * h : 4 * h + 4].rearrange("p b n t -> p (b n t)"),
+                )
+
+            def stage2_mm(k, b):
+                yc, ys = state[("yc", k)]
+                ps = psv.tile([P, C], F32, name="pv")
+                nc.tensor.matmul_mx(
+                    out=ps[:],
+                    lhsT=yc[:, P * b : P * b + P].bitcast(E4M3),
+                    lhsT_scale=ys[:, P * b : P * b + P],
+                    rhs=w2[:, b, :].bitcast(E2M1),
+                    rhs_scale=w2s[:, b, :],
+                    start=True,
+                    stop=True,
+                )
+                state[("p2", k, b)] = ps
+
+            def stage2_exit(k, b):
+                if b == 0:
+                    ztile = work.tile([P, FR, NB, 64], BF16, name="z", align_bytes=64)
+                    state[("z", k)] = ztile
+                nc.vector.tensor_tensor(
+                    out=state[("z", k)][:, :, b, :],
+                    in0=state[("p2", k, b)][:].rearrange("p (f d) -> p f d", f=FR),
+                    in1=state[("y2", k, b)][:].rearrange("p (f d) -> p f d", f=FR),
+                    op=ALU.add,
+                )
+
+            def z_turn(k, g):
+                zw = state[("z", k)][:].rearrange("p f b d -> p (f b d)").bitcast(F32)
+                ps = pss.tile([P, 4, P], F32, name="pt")
+                for i in range(4):
+                    f, u = 2 * g + i // 2, i % 2
+                    nc.tensor.transpose(
+                        ps[:, i, :], zw[:, 256 * f + u : 256 * f + 256 : 2], ident[:]
+                    )
+                state[("pz", k, g)] = ps
+
+            def z_turn_exit(k, g, eng):
+                if g == 0:
+                    ztile = work.tile([P, FR, P, 4], BF16, name="zT", align_bytes=64)
+                    state[("zT", k)] = ztile
+                words = state[("zT", k)][:].rearrange("p f n t -> p (f n t)").bitcast(F32)
+                dst = words[:, 512 * g : 512 * g + 512].rearrange("p (f n u) -> p f n u", f=2, u=2)
+                src = state[("pz", k, g)][:].rearrange("p (f u) n -> p f n u", u=2)
+                if eng == "v":
+                    nc.vector.tensor_copy(out=dst, in_=src)
+                else:
+                    nc.scalar.copy(out=dst, in_=src)
+
+            def quant_z(k, h):
+                if h == 0:
+                    zc = work.tile([P, FR * P], U32, name="zc", align_bytes=64)
+                    zs = work.tile([P, FR * P], U8, name="zs", align_bytes=64)
+                    state[("zc", k)] = (zc, zs)
+                zc, zs = state[("zc", k)]
+                nc.vector.quantize_mx(
+                    out=zc[:, 512 * h : 512 * h + 512].bitcast(E4M3),
+                    scales=zs[:, 512 * h : 512 * h + 512],
+                    in_=state[("zT", k)][:, 4 * h : 4 * h + 4].rearrange("p f n t -> p (f n t)"),
+                )
+
+            def stage3(k, f, eng):
+                zc, zs = state[("zc", k)]
+                ps = pss.tile([P, C], F32, name="pt") if eng == "s" else psv.tile([P, C], F32, name="pv")
+                nc.tensor.matmul_mx(
+                    out=ps[:],
+                    lhsT=zc[:, P * f : P * f + P].bitcast(E4M3),
+                    lhsT_scale=zs[:, P * f : P * f + P],
+                    rhs=w3[:].bitcast(E2M1),
+                    rhs_scale=w3s[:],
+                    start=True,
+                    stop=True,
+                )
+                o = outs.tile([P, C], F32, name="o", align_bytes=64)
+                if eng == "s":
+                    nc.scalar.activation(
+                        out=o[:], in_=ps[:], func=ACT.Copy, scale=gate[:, f, k : k + 1]
+                    )
+                else:
+                    nc.vector.tensor_scalar(
+                        out=o[:], in0=ps[:], scalar1=gate[:, f, k : k + 1], scalar2=None, op0=ALU.mult
+                    )
+                nc.sync.dma_start(
+                    out=out[f].rearrange("(p j) o -> p j o", j=4)[:, k, :], in_=o[:]
+                )
+
+            for i in range(FR + 2):
+                if i < FR:
+                    cut = 2 if i % 2 == 0 else 1
+                    interleave(i, "v", 0, cut)
+                    interleave(i, "s", cut, 4)
+                if i == 2:
+                    nc.scalar.activation(
+                        out=gate[:].rearrange("p f j -> p (f j)"),
+                        in_=sp[:].rearrange("p f j -> p (f j)"),
+                        func=ACT.Tanh,
+                    )
+                if 1 <= i <= FR:
+                    quant_x(i - 1)
+                    stage1_mm(0, i - 1)
+                if i >= 2:
+                    stage1_exit(0, i - 2)
+            for b in range(NB):
+                skip_y(0, b)
+
+            for k in range(5):
+                if k < 3:
+                    stage1_mm(k + 1, 0)
+                    stage1_mm(k + 1, 1)
+                if k > 0:
+                    for g in range(4):
+                        z_turn(k - 1, g)
+                        z_turn_exit(k - 1, g, "s" if k < 4 or g % 2 == 0 else "v")
+                if k < 3:
+                    for f in range(4):
+                        if f >= 2:
+                            stage1_mm(k + 1, f)
+                        stage1_exit(k + 1, f)
+                if k < 4:
+                    for b in range(4):
+                        y_turn(k, b)
+                        y_turn_exit(k, b)
+                if k > 0:
+                    quant_z(k - 1, 0)
+                    quant_z(k - 1, 1)
+                if k < 3:
+                    for f in range(4, FR):
+                        stage1_mm(k + 1, f)
+                        stage1_exit(k + 1, f)
+                if k < 4:
+                    for b in range(4, NB):
+                        y_turn(k, b)
+                        y_turn_exit(k, b)
+                    quant_y(k, 0)
+                    for b in range(4):
+                        stage2_mm(k, b)
+                        stage2_exit(k, b)
+                if k > 0:
+                    for f in range(4):
+                        stage3(k - 1, f, "s" if k < 4 or f % 2 == 0 else "v")
+                if k < 4:
+                    quant_y(k, 1)
+                    for b in range(4, NB):
+                        stage2_mm(k, b)
+                        stage2_exit(k, b)
+                if k > 0:
+                    for f in range(4, FR):
+                        stage3(k - 1, f, "s" if k < 4 or f % 2 == 0 else "v")
+                if k < 3:
+                    for b in range(NB):
+                        skip_y(k + 1, b)

@@ -28,8 +28,10 @@ def tile_video_token_mixer_t2_kernel(
         keep = ctx.enter_context(tc.tile_pool(name="keep", bufs=1))
         raws = ctx.enter_context(tc.tile_pool(name="raws", bufs=5))
         work = ctx.enter_context(tc.tile_pool(name="work", bufs=2))
-        y2s = ctx.enter_context(tc.tile_pool(name="y2s", bufs=10))
-        outs = ctx.enter_context(tc.tile_pool(name="outs", bufs=6))
+        ys3 = ctx.enter_context(tc.tile_pool(name="ys3", bufs=3))
+        once = ctx.enter_context(tc.tile_pool(name="once", bufs=1))
+        y2s = ctx.enter_context(tc.tile_pool(name="y2s", bufs=6))
+        outs = ctx.enter_context(tc.tile_pool(name="outs", bufs=9))
         psv = ctx.enter_context(tc.psum_pool(name="psv", bufs=4))
         pss = ctx.enter_context(tc.psum_pool(name="pss", bufs=4))
 
@@ -57,21 +59,22 @@ def tile_video_token_mixer_t2_kernel(
             nc.vector.memset(warm[:], 0.0)
             nc.vector.memset(w2s[:].rearrange("p b n -> p (b n)").bitcast(I32), 0)
             nc.vector.memset(w3s[:].bitcast(I32), 0)
+            for q in range(4):
+                nc.scalar.dma_start(
+                    out=w1s_raw[32 * q : 32 * q + 4, :].bitcast(I32),
+                    in_=w1_scales[0, 4 * q : 4 * q + 4, :].bitcast(I32),
+                )
+            nc.scalar.dma_start(out=s1[:], in_=skip1.rearrange("(p j) -> p j", j=4))
+            nc.scalar.dma_start(out=sp[:], in_=speed.rearrange("f (p j) -> p f j", j=4))
             nc.scalar.activation(out=warm[:], in_=warm[:], func=ACT.Tanh)
-            nc.sync.dma_start(out=w1_raw[:].bitcast(I32), in_=w1_words[0].bitcast(I32))
+            make_identity(nc, ident[:])
             xr = []
             for f in range(FR):
                 t = raws.tile([P, 4, C], BF16, name="xraw", align_bytes=64)
                 nc.sync.dma_start(out=t[:], in_=x[f].rearrange("(p j) c -> p j c", j=4))
                 xr.append(t)
-            for q in range(4):
-                nc.gpsimd.dma_start(
-                    out=w1s_raw[32 * q : 32 * q + 4, :].bitcast(I32),
-                    in_=w1_scales[0, 4 * q : 4 * q + 4, :].bitcast(I32),
-                )
-            nc.gpsimd.dma_start(out=s1[:], in_=skip1.rearrange("(p j) -> p j", j=4))
-            nc.gpsimd.dma_start(out=sp[:], in_=speed.rearrange("f (p j) -> p f j", j=4))
-            make_identity(nc, ident[:])
+                if f == 0:
+                    nc.sync.dma_start(out=w1_raw[:].bitcast(I32), in_=w1_words[0].bitcast(I32))
             nc.sync.dma_start(
                 out=s2[:].rearrange("p f c -> p (f c)"),
                 in_=skip2.rearrange("f c -> (f c)").partition_broadcast(P),
@@ -80,33 +83,36 @@ def tile_video_token_mixer_t2_kernel(
                 out=w2[:].bitcast(I32), in_=w2_words.rearrange("g p n -> p g n").bitcast(I32)
             )
             for q in range(4):
-                nc.gpsimd.dma_start(
+                nc.sync.dma_start(
                     out=w2s[32 * q : 32 * q + 4, :, :].bitcast(I32),
                     in_=w2_scales[:, 4 * q : 4 * q + 4, :].rearrange("g r n -> r g n").bitcast(I32),
                 )
             nc.sync.dma_start(out=w3[:].bitcast(I32), in_=w3_words[0].bitcast(I32))
             for q in range(4):
-                nc.gpsimd.dma_start(
+                nc.sync.dma_start(
                     out=w3s[32 * q : 32 * q + 4, :].bitcast(I32),
                     in_=w3_scales[0, 4 * q : 4 * q + 4, :].bitcast(I32),
                 )
 
-            nc.vector.tensor_copy(
-                out=w1s[:], in_=w1s_raw[:].rearrange("p (m j) -> p j m", j=4)
-            )
-            nc.vector.tensor_copy(
-                out=w1[:].rearrange("p j (m e) -> p j m e", e=2),
-                in_=w1_raw[:].rearrange("p (m j e) -> p j m e", j=4, e=2),
-            )
-            nc.vector.tensor_copy(out=s1f[:], in_=s1[:])
+            def group_w1(j0, j1):
+                nc.vector.tensor_copy(
+                    out=w1s[:, j0:j1], in_=w1s_raw[:].rearrange("p (m j) -> p j m", j=4)[:, j0:j1]
+                )
+                nc.vector.tensor_copy(
+                    out=w1[:].rearrange("p j (m e) -> p j m e", e=2)[:, j0:j1],
+                    in_=w1_raw[:].rearrange("p (m j e) -> p j m e", j=4, e=2)[:, j0:j1],
+                )
 
             def interleave(f, eng, t0, t1):
-                dst = xg[f][:].rearrange("p (t a) j -> p t a j", t=4)[:, t0:t1]
-                src = xr[f][:].rearrange("p j (a t) -> p t a j", t=4)[:, t0:t1]
-                if t1 - t0 == 1:
-                    dst, src = dst[:, 0], src[:, 0]
+                a0, a1 = 32 * t0, 32 * t1
+                dst = xg[f][:].rearrange("p (t a) j -> p a j t", t=4)[:, a0:a1]
+                src = xr[f][:].rearrange("p j (a t) -> p a j t", t=4)[:, a0:a1]
                 if eng == "v":
                     nc.vector.tensor_copy(out=dst, in_=src)
+                elif eng == "g":
+                    nc.gpsimd.tensor_scalar(
+                        out=dst, in0=src, scalar1=1.0, scalar2=0.0, op0=ALU.mult, op1=ALU.add
+                    )
                 else:
                     nc.scalar.copy(out=dst, in_=src)
 
@@ -133,8 +139,8 @@ def tile_video_token_mixer_t2_kernel(
                 state[("p1", k, f)] = ps
 
             def stage1_exit(k, f):
-                if f == 0:
-                    ytile = work.tile([P, 32, P], F32, name="y", align_bytes=64)
+                if ("y", k) not in state:
+                    ytile = ys3.tile([P, 32, P], F32, name="y", align_bytes=64)
                     state[("y", k)] = ytile
                 y = state[("y", k)]
                 nc.vector.scalar_tensor_tensor(
@@ -146,16 +152,17 @@ def tile_video_token_mixer_t2_kernel(
                     op1=ALU.add,
                 )
 
-            def skip_y(k, b):
-                y2 = y2s.tile([P, C], F32, name="y2", align_bytes=64)
+            def skip_y(k, b, eng):
+                if ("y2", k, b // 2) not in state:
+                    y2 = y2s.tile([P, 2, C], F32, name="y2", align_bytes=64)
+                    state[("y2", k, b // 2)] = y2
                 y = state[("y", k)]
-                nc.gpsimd.tensor_tensor(
-                    out=y2[:].rearrange("p (f q t) -> p f q t", f=FR, t=4),
+                eng.tensor_tensor(
+                    out=state[("y2", k, b // 2)][:, b % 2].rearrange("p (f q t) -> p f q t", f=FR, t=4),
                     in0=y[:].rearrange("p (t b) (f q) -> p b f q t", t=4, q=16)[:, b],
                     in1=s2[:, :, 64 * b : 64 * b + 64].rearrange("p f (q t) -> p f q t", t=4),
                     op=ALU.mult,
                 )
-                state[("y2", k, b)] = y2
 
             def y_turn(k, b):
                 y = state[("y", k)]
@@ -164,17 +171,19 @@ def tile_video_token_mixer_t2_kernel(
                     nc.tensor.transpose(ps[:, t, :], y[:, 8 * t + b, :], ident[:])
                 state[("pt", k, b)] = ps
 
-            def y_turn_exit(k, b):
-                if b == 0:
-                    ytile = work.tile([P, NB, P, 4], BF16, name="yT", align_bytes=64)
+            def y_turn_exit(k, b, eng):
+                if ("yT", k) not in state:
+                    ytile = once.tile([P, NB, P, 4], BF16, name="yT", align_bytes=64)
                     state[("yT", k)] = ytile
-                nc.scalar.copy(
-                    out=state[("yT", k)][:, b],
-                    in_=state[("pt", k, b)][:].rearrange("p t n -> p n t"),
-                )
+                dst = state[("yT", k)][:, b]
+                src = state[("pt", k, b)][:].rearrange("p t n -> p n t")
+                if eng == "v":
+                    nc.vector.tensor_copy(out=dst, in_=src)
+                else:
+                    nc.scalar.copy(out=dst, in_=src)
 
             def quant_y(k, h):
-                if h == 0:
+                if ("yc", k) not in state:
                     yc = work.tile([P, NB * P], U32, name="yc", align_bytes=64)
                     ys = work.tile([P, NB * P], U8, name="ys", align_bytes=64)
                     state[("yc", k)] = (yc, ys)
@@ -185,28 +194,30 @@ def tile_video_token_mixer_t2_kernel(
                     in_=state[("yT", k)][:, 4 * h : 4 * h + 4].rearrange("p b n t -> p (b n t)"),
                 )
 
-            def stage2_mm(k, b):
+            def stage2_mm(k, m, h):
                 yc, ys = state[("yc", k)]
-                ps = psv.tile([P, C], F32, name="pv")
-                nc.tensor.matmul_mx(
-                    out=ps[:],
-                    lhsT=yc[:, P * b : P * b + P].bitcast(E4M3),
-                    lhsT_scale=ys[:, P * b : P * b + P],
-                    rhs=w2[:, b, :].bitcast(E2M1),
-                    rhs_scale=w2s[:, b, :],
-                    start=True,
-                    stop=True,
-                )
-                state[("p2", k, b)] = ps
+                ps = psv.tile([P, 2, C // 2], F32, name="pv")
+                for i in range(2):
+                    b = 2 * m + i
+                    nc.tensor.matmul_mx(
+                        out=ps[:, i, :],
+                        lhsT=yc[:, P * b : P * b + P].bitcast(E4M3),
+                        lhsT_scale=ys[:, P * b : P * b + P],
+                        rhs=w2[:, b, 512 * h : 512 * h + 512].bitcast(E2M1),
+                        rhs_scale=w2s[:, b, 256 * h : 256 * h + 256],
+                        start=True,
+                        stop=True,
+                    )
+                state[("p2", k, m, h)] = ps
 
-            def stage2_exit(k, b):
-                if b == 0:
-                    ztile = work.tile([P, FR, NB, 64], BF16, name="z", align_bytes=64)
+            def stage2_exit(k, m, h):
+                if ("z", k) not in state:
+                    ztile = once.tile([P, FR, NB, 64], BF16, name="z", align_bytes=64)
                     state[("z", k)] = ztile
                 nc.vector.tensor_tensor(
-                    out=state[("z", k)][:, :, b, :],
-                    in0=state[("p2", k, b)][:].rearrange("p (f d) -> p f d", f=FR),
-                    in1=state[("y2", k, b)][:].rearrange("p (f d) -> p f d", f=FR),
+                    out=state[("z", k)][:, 4 * h : 4 * h + 4, 2 * m : 2 * m + 2, :].rearrange("p f b d -> p b f d"),
+                    in0=state[("p2", k, m, h)][:].rearrange("p b (f d) -> p b f d", f=4),
+                    in1=state[("y2", k, m)][:, :, 256 * h : 256 * h + 256].rearrange("p b (f d) -> p b f d", f=4),
                     op=ALU.add,
                 )
 
@@ -221,8 +232,8 @@ def tile_video_token_mixer_t2_kernel(
                 state[("pz", k, g)] = ps
 
             def z_turn_exit(k, g, eng):
-                if g == 0:
-                    ztile = work.tile([P, FR, P, 4], BF16, name="zT", align_bytes=64)
+                if ("zT", k) not in state:
+                    ztile = once.tile([P, FR, P, 4], BF16, name="zT", align_bytes=64)
                     state[("zT", k)] = ztile
                 words = state[("zT", k)][:].rearrange("p f n t -> p (f n t)").bitcast(F32)
                 dst = words[:, 512 * g : 512 * g + 512].rearrange("p (f n u) -> p f n u", f=2, u=2)
@@ -233,7 +244,7 @@ def tile_video_token_mixer_t2_kernel(
                     nc.scalar.copy(out=dst, in_=src)
 
             def quant_z(k, h):
-                if h == 0:
+                if ("zc", k) not in state:
                     zc = work.tile([P, FR * P], U32, name="zc", align_bytes=64)
                     zs = work.tile([P, FR * P], U8, name="zs", align_bytes=64)
                     state[("zc", k)] = (zc, zs)
@@ -244,9 +255,9 @@ def tile_video_token_mixer_t2_kernel(
                     in_=state[("zT", k)][:, 4 * h : 4 * h + 4].rearrange("p f n t -> p (f n t)"),
                 )
 
-            def stage3(k, f, eng):
+            def stage3_mm(k, f):
                 zc, zs = state[("zc", k)]
-                ps = pss.tile([P, C], F32, name="pt") if eng == "s" else psv.tile([P, C], F32, name="pv")
+                ps = pss.tile([P, C], F32, name="pt")
                 nc.tensor.matmul_mx(
                     out=ps[:],
                     lhsT=zc[:, P * f : P * f + P].bitcast(E4M3),
@@ -256,6 +267,10 @@ def tile_video_token_mixer_t2_kernel(
                     start=True,
                     stop=True,
                 )
+                state[("p3", k, f)] = ps
+
+            def stage3_exit(k, f, eng):
+                ps = state[("p3", k, f)]
                 o = outs.tile([P, C], F32, name="o", align_bytes=64)
                 if eng == "s":
                     nc.scalar.activation(
@@ -269,68 +284,373 @@ def tile_video_token_mixer_t2_kernel(
                     out=out[f].rearrange("(p j) o -> p j o", j=4)[:, k, :], in_=o[:]
                 )
 
-            for i in range(FR + 2):
-                if i < FR:
-                    cut = 2 if i % 2 == 0 else 1
-                    interleave(i, "v", 0, cut)
-                    interleave(i, "s", cut, 4)
-                if i == 2:
-                    nc.scalar.activation(
-                        out=gate[:].rearrange("p f j -> p (f j)"),
-                        in_=sp[:].rearrange("p f j -> p (f j)"),
-                        func=ACT.Tanh,
-                    )
-                if 1 <= i <= FR:
-                    quant_x(i - 1)
-                    stage1_mm(0, i - 1)
-                if i >= 2:
-                    stage1_exit(0, i - 2)
-            for b in range(NB):
-                skip_y(0, b)
+            def gate_tanh():
+                nc.scalar.activation(
+                    out=gate[:].rearrange("p f j -> p (f j)"),
+                    in_=sp[:].rearrange("p f j -> p (f j)"),
+                    func=ACT.Tanh,
+                )
 
-            for k in range(5):
-                if k < 3:
-                    stage1_mm(k + 1, 0)
-                    stage1_mm(k + 1, 1)
-                if k > 0:
-                    for g in range(4):
-                        z_turn(k - 1, g)
-                        z_turn_exit(k - 1, g, "s" if k < 4 or g % 2 == 0 else "v")
-                if k < 3:
-                    for f in range(4):
-                        if f >= 2:
-                            stage1_mm(k + 1, f)
-                        stage1_exit(k + 1, f)
-                if k < 4:
-                    for b in range(4):
-                        y_turn(k, b)
-                        y_turn_exit(k, b)
-                if k > 0:
-                    quant_z(k - 1, 0)
-                    quant_z(k - 1, 1)
-                if k < 3:
-                    for f in range(4, FR):
-                        stage1_mm(k + 1, f)
-                        stage1_exit(k + 1, f)
-                if k < 4:
-                    for b in range(4, NB):
-                        y_turn(k, b)
-                        y_turn_exit(k, b)
-                    quant_y(k, 0)
-                    for b in range(4):
-                        stage2_mm(k, b)
-                        stage2_exit(k, b)
-                if k > 0:
-                    for f in range(4):
-                        stage3(k - 1, f, "s" if k < 4 or f % 2 == 0 else "v")
-                if k < 4:
-                    quant_y(k, 1)
-                    for b in range(4, NB):
-                        stage2_mm(k, b)
-                        stage2_exit(k, b)
-                if k > 0:
-                    for f in range(4, FR):
-                        stage3(k - 1, f, "s" if k < 4 or f % 2 == 0 else "v")
-                if k < 3:
-                    for b in range(NB):
-                        skip_y(k + 1, b)
+            interleave(0, "v", 0, 1)
+            interleave(0, "s", 1, 3)
+            interleave(0, "g", 3, 4)
+            group_w1(0, 1); nc.vector.tensor_copy(out=s1f[:], in_=s1[:])
+            interleave(1, "v", 0, 1)
+            interleave(1, "s", 1, 4)
+            group_w1(1, 4)
+            quant_x(0)
+            stage1_mm(0, 0)
+            stage1_mm(1, 0)
+            interleave(2, "v", 0, 1)
+            interleave(2, "s", 1, 3)
+            interleave(2, "g", 3, 4)
+            quant_x(1)
+            stage1_mm(0, 1)
+            stage1_mm(1, 1)
+            stage1_exit(0, 0)
+            stage1_exit(1, 0)
+            interleave(3, "s", 0, 3)
+            interleave(3, "g", 3, 4)
+            quant_x(2); gate_tanh()
+            stage1_mm(0, 2)
+            stage1_mm(1, 2)
+            stage1_exit(0, 1)
+            stage1_exit(1, 1)
+            interleave(4, "s", 0, 4)
+            quant_x(3)
+            stage1_mm(0, 3)
+            stage1_mm(1, 3)
+            stage1_exit(0, 2)
+            stage1_exit(1, 2)
+            interleave(5, "s", 0, 3)
+            interleave(5, "g", 3, 4)
+            quant_x(4)
+            stage1_mm(0, 4)
+            stage1_mm(1, 4)
+            stage1_exit(0, 3)
+            stage1_exit(1, 3)
+            interleave(6, "s", 0, 3)
+            interleave(6, "g", 3, 4)
+            quant_x(5)
+            stage1_mm(0, 5)
+            stage1_mm(1, 5)
+            stage1_exit(0, 4)
+            stage1_exit(1, 4)
+            interleave(7, "s", 0, 3)
+            interleave(7, "g", 3, 4)
+            quant_x(6)
+            stage1_mm(0, 6)
+            stage1_mm(1, 6)
+            stage1_exit(0, 5)
+            stage1_exit(1, 5)
+            quant_x(7)
+            stage1_mm(0, 7)
+            stage1_mm(1, 7)
+            stage1_exit(0, 6)
+            stage1_exit(1, 6)
+            stage1_exit(0, 7)
+            stage1_exit(1, 7)
+            skip_y(0, 0, nc.vector)
+            stage1_mm(2, 3)
+            stage1_mm(2, 0)
+            stage1_exit(2, 3)
+            y_turn(0, 3)
+            y_turn(0, 4)
+            y_turn_exit(0, 3, "s")
+            skip_y(0, 6, nc.gpsimd)
+            skip_y(0, 1, nc.gpsimd)
+            stage1_mm(2, 2)
+            y_turn_exit(0, 4, "s")
+            y_turn(0, 0)
+            stage1_mm(2, 4)
+            stage1_exit(2, 2)
+            y_turn(0, 2)
+            stage1_exit(2, 0)
+            y_turn_exit(0, 0, "s")
+            y_turn(0, 1)
+            y_turn_exit(0, 2, "v")
+            skip_y(0, 5, nc.gpsimd)
+            stage1_mm(2, 5)
+            stage1_exit(2, 4)
+            y_turn_exit(0, 1, "s")
+            y_turn(0, 6)
+            stage1_mm(2, 1)
+            stage1_exit(2, 5)
+            y_turn_exit(0, 6, "s")
+            skip_y(0, 7, nc.gpsimd)
+            stage1_exit(2, 1)
+            y_turn(0, 7)
+            skip_y(0, 2, nc.vector)
+            y_turn(0, 5)
+            y_turn_exit(0, 7, "s")
+            stage1_mm(2, 7)
+            quant_y(0, 0)
+            y_turn_exit(0, 5, "s")
+            stage1_mm(2, 6)
+            stage2_mm(0, 0, 0)
+            stage1_exit(2, 7)
+            stage1_exit(2, 6)
+            skip_y(0, 3, nc.gpsimd)
+            stage2_mm(0, 1, 0)
+            quant_y(0, 1)
+            stage2_exit(0, 1, 0)
+            stage2_mm(0, 3, 0)
+            stage2_exit(0, 0, 0)
+            stage2_mm(0, 2, 0)
+            stage2_exit(0, 3, 0)
+            skip_y(0, 4, nc.gpsimd)
+            stage2_mm(0, 1, 1)
+            stage2_mm(0, 3, 1)
+            stage2_mm(0, 0, 1)
+            stage2_exit(0, 2, 0)
+            stage2_exit(0, 1, 1)
+            stage2_exit(0, 3, 1)
+            stage2_mm(0, 2, 1)
+            stage2_exit(0, 2, 1)
+            z_turn(0, 1)
+            stage2_exit(0, 0, 1)
+            skip_y(1, 0, nc.gpsimd)
+            stage1_mm(3, 3)
+            stage1_mm(3, 0)
+            z_turn_exit(0, 1, "s")
+            z_turn(0, 0)
+            stage1_exit(3, 3)
+            y_turn(1, 3)
+            y_turn(1, 4)
+            z_turn_exit(0, 0, "v")
+            y_turn_exit(1, 3, "s")
+            skip_y(1, 6, nc.gpsimd)
+            skip_y(1, 1, nc.vector)
+            z_turn(0, 2)
+            stage1_mm(3, 2)
+            y_turn_exit(1, 4, "s")
+            quant_z(0, 0)
+            z_turn(0, 3)
+            y_turn(1, 0)
+            stage1_mm(3, 4)
+            stage1_exit(3, 2)
+            y_turn(1, 2)
+            z_turn_exit(0, 2, "s")
+            stage1_exit(3, 0)
+            z_turn_exit(0, 3, "s")
+            y_turn_exit(1, 0, "s")
+            y_turn(1, 1)
+            y_turn_exit(1, 2, "s")
+            skip_y(1, 5, nc.gpsimd)
+            stage1_mm(3, 5)
+            quant_z(0, 1)
+            stage1_exit(3, 4)
+            y_turn_exit(1, 1, "s")
+            y_turn(1, 6)
+            stage1_mm(3, 1)
+            stage1_exit(3, 5)
+            y_turn_exit(1, 6, "v")
+            skip_y(1, 7, nc.gpsimd)
+            stage1_exit(3, 1)
+            y_turn(1, 7)
+            skip_y(1, 2, nc.gpsimd)
+            y_turn(1, 5)
+            y_turn_exit(1, 7, "s")
+            stage1_mm(3, 7)
+            stage3_mm(0, 0)
+            quant_y(1, 0)
+            stage3_mm(0, 1)
+            y_turn_exit(1, 5, "s")
+            stage3_mm(0, 5)
+            stage3_exit(0, 0, "s")
+            stage1_mm(3, 6)
+            stage3_exit(0, 1, "s")
+            stage2_mm(1, 0, 0)
+            stage1_exit(3, 7)
+            stage1_exit(3, 6)
+            skip_y(1, 3, nc.gpsimd)
+            stage2_mm(1, 1, 0)
+            stage3_exit(0, 5, "s")
+            stage3_mm(0, 6)
+            stage3_mm(0, 3)
+            quant_y(1, 1)
+            stage2_exit(1, 1, 0)
+            stage2_mm(1, 3, 0)
+            stage3_mm(0, 7)
+            stage2_exit(1, 0, 0)
+            stage2_mm(1, 2, 0)
+            stage2_exit(1, 3, 0)
+            stage3_exit(0, 6, "s")
+            skip_y(1, 4, nc.gpsimd)
+            stage3_exit(0, 3, "s")
+            stage3_exit(0, 7, "s")
+            stage3_mm(0, 4)
+            stage2_mm(1, 1, 1)
+            stage3_exit(0, 4, "s")
+            stage2_mm(1, 3, 1)
+            stage2_mm(1, 0, 1)
+            stage3_mm(0, 2)
+            stage2_exit(1, 2, 0)
+            stage2_exit(1, 1, 1)
+            stage2_exit(1, 3, 1)
+            stage2_mm(1, 2, 1)
+            stage2_exit(1, 2, 1)
+            z_turn(1, 1)
+            stage2_exit(1, 0, 1)
+            skip_y(2, 0, nc.gpsimd)
+            stage3_exit(0, 2, "s")
+            z_turn_exit(1, 1, "s")
+            z_turn(1, 0)
+            y_turn(2, 3)
+            y_turn(2, 4)
+            z_turn_exit(1, 0, "s")
+            y_turn_exit(2, 3, "s")
+            skip_y(2, 6, nc.gpsimd)
+            skip_y(2, 1, nc.gpsimd)
+            z_turn(1, 2)
+            y_turn_exit(2, 4, "v")
+            quant_z(1, 0)
+            z_turn(1, 3)
+            y_turn(2, 0)
+            y_turn(2, 2)
+            z_turn_exit(1, 2, "s")
+            z_turn_exit(1, 3, "s")
+            y_turn_exit(2, 0, "v")
+            y_turn(2, 1)
+            y_turn_exit(2, 2, "v")
+            skip_y(2, 5, nc.gpsimd)
+            quant_z(1, 1)
+            y_turn_exit(2, 1, "v")
+            y_turn(2, 6)
+            y_turn_exit(2, 6, "s")
+            skip_y(2, 7, nc.gpsimd)
+            y_turn(2, 7)
+            skip_y(2, 2, nc.vector)
+            y_turn(2, 5)
+            y_turn_exit(2, 7, "s")
+            stage3_mm(1, 0)
+            quant_y(2, 0)
+            stage3_mm(1, 1)
+            y_turn_exit(2, 5, "v")
+            stage3_mm(1, 5)
+            stage3_exit(1, 0, "v")
+            stage3_exit(1, 1, "s")
+            stage2_mm(2, 0, 0)
+            skip_y(2, 3, nc.gpsimd)
+            stage2_mm(2, 1, 0)
+            stage3_exit(1, 5, "s")
+            stage3_mm(1, 6)
+            stage3_mm(1, 3)
+            quant_y(2, 1)
+            stage2_exit(2, 1, 0)
+            stage2_mm(2, 3, 0)
+            stage3_mm(1, 7)
+            stage2_exit(2, 0, 0)
+            stage2_mm(2, 2, 0)
+            stage2_exit(2, 3, 0)
+            stage3_exit(1, 6, "s")
+            skip_y(2, 4, nc.gpsimd)
+            stage3_exit(1, 3, "s")
+            stage3_exit(1, 7, "s")
+            stage3_mm(1, 4)
+            stage2_mm(2, 1, 1)
+            stage3_exit(1, 4, "s")
+            stage2_mm(2, 3, 1)
+            stage2_mm(2, 0, 1)
+            stage3_mm(1, 2)
+            stage2_exit(2, 2, 0)
+            stage2_exit(2, 1, 1)
+            stage2_exit(2, 3, 1)
+            stage2_mm(2, 2, 1)
+            stage2_exit(2, 2, 1)
+            z_turn(2, 1)
+            stage2_exit(2, 0, 1)
+            skip_y(3, 0, nc.gpsimd)
+            stage3_exit(1, 2, "s")
+            z_turn_exit(2, 1, "s")
+            z_turn(2, 0)
+            y_turn(3, 3)
+            y_turn(3, 4)
+            z_turn_exit(2, 0, "s")
+            y_turn_exit(3, 3, "v")
+            skip_y(3, 6, nc.gpsimd)
+            skip_y(3, 1, nc.gpsimd)
+            z_turn(2, 2)
+            y_turn_exit(3, 4, "v")
+            quant_z(2, 0)
+            z_turn(2, 3)
+            y_turn(3, 0)
+            y_turn(3, 2)
+            z_turn_exit(2, 2, "s")
+            z_turn_exit(2, 3, "v")
+            y_turn_exit(3, 0, "s")
+            y_turn(3, 1)
+            y_turn_exit(3, 2, "s")
+            skip_y(3, 5, nc.gpsimd)
+            quant_z(2, 1)
+            y_turn_exit(3, 1, "s")
+            y_turn(3, 6)
+            y_turn_exit(3, 6, "s")
+            skip_y(3, 7, nc.vector)
+            y_turn(3, 7)
+            skip_y(3, 2, nc.vector)
+            y_turn(3, 5)
+            y_turn_exit(3, 7, "s")
+            stage3_mm(2, 0)
+            quant_y(3, 0)
+            stage3_mm(2, 1)
+            y_turn_exit(3, 5, "s")
+            stage3_mm(2, 5)
+            stage3_exit(2, 0, "s")
+            stage3_exit(2, 1, "s")
+            stage2_mm(3, 0, 0)
+            skip_y(3, 3, nc.gpsimd)
+            stage2_mm(3, 1, 0)
+            stage3_exit(2, 5, "s")
+            stage3_mm(2, 6)
+            stage3_mm(2, 3)
+            quant_y(3, 1)
+            stage2_exit(3, 1, 0)
+            stage2_mm(3, 3, 0)
+            stage3_mm(2, 7)
+            stage2_exit(3, 0, 0)
+            stage2_mm(3, 2, 0)
+            stage2_exit(3, 3, 0)
+            stage3_exit(2, 6, "s")
+            skip_y(3, 4, nc.gpsimd)
+            stage3_exit(2, 3, "s")
+            stage3_exit(2, 7, "s")
+            stage3_mm(2, 4)
+            stage2_mm(3, 1, 1)
+            stage3_exit(2, 4, "s")
+            stage2_mm(3, 3, 1)
+            stage2_mm(3, 0, 1)
+            stage3_mm(2, 2)
+            stage2_exit(3, 2, 0)
+            stage2_exit(3, 1, 1)
+            stage2_exit(3, 3, 1)
+            stage2_mm(3, 2, 1)
+            stage2_exit(3, 2, 1)
+            z_turn(3, 1)
+            stage2_exit(3, 0, 1)
+            stage3_exit(2, 2, "s")
+            z_turn_exit(3, 1, "s")
+            z_turn(3, 0)
+            z_turn_exit(3, 0, "s")
+            z_turn(3, 2)
+            quant_z(3, 0)
+            z_turn(3, 3)
+            z_turn_exit(3, 2, "v")
+            z_turn_exit(3, 3, "s")
+            quant_z(3, 1)
+            stage3_mm(3, 0)
+            stage3_mm(3, 1)
+            stage3_mm(3, 5)
+            stage3_exit(3, 0, "s")
+            stage3_exit(3, 1, "s")
+            stage3_exit(3, 5, "v")
+            stage3_mm(3, 6)
+            stage3_mm(3, 3)
+            stage3_mm(3, 7)
+            stage3_exit(3, 6, "s")
+            stage3_exit(3, 3, "v")
+            stage3_exit(3, 7, "s")
+            stage3_mm(3, 4)
+            stage3_exit(3, 4, "s")
+            stage3_mm(3, 2)
+            stage3_exit(3, 2, "v")

from contextlib import ExitStack

import concourse.mybir as mybir
from concourse.masks import make_identity

F32 = mybir.dt.float32
BF16 = mybir.dt.bfloat16
I32 = mybir.dt.int32
U32 = mybir.dt.uint32
U8 = mybir.dt.uint8
E4M3 = mybir.dt.float8_e4m3fn_x4
E2M1 = mybir.dt.float4_e2m1fn_x4
ALU = mybir.AluOpType
ACT = mybir.ActivationFunctionType

P = 128
FR = 8
NB = 8
C = 512
FLOPS = 3 * 2 * 8 * 512 * 512 * 512


def tile_video_token_mixer_t2_kernel(
    tc, x, w1_words, w1_scales, w2_words, w2_scales, w3_words, w3_scales, skip1, skip2, speed, out
):
    nc = tc.nc
    with ExitStack() as ctx:
        keep = ctx.enter_context(tc.tile_pool(name="keep", bufs=1))
        raws = ctx.enter_context(tc.tile_pool(name="raws", bufs=5))
        work = ctx.enter_context(tc.tile_pool(name="work", bufs=2))
        ys3 = ctx.enter_context(tc.tile_pool(name="ys3", bufs=3))
        once = ctx.enter_context(tc.tile_pool(name="once", bufs=1))
        y2s = ctx.enter_context(tc.tile_pool(name="y2s", bufs=6))
        outs = ctx.enter_context(tc.tile_pool(name="outs", bufs=9))
        psv = ctx.enter_context(tc.psum_pool(name="psv", bufs=4))
        pss = ctx.enter_context(tc.psum_pool(name="pss", bufs=4))

        w1_raw = keep.tile([P, 1024], U8, name="w1_raw", align_bytes=64)
        w1s_raw = keep.tile([P, 512], U8, name="w1s_raw", align_bytes=64)
        w1 = keep.tile([P, 4, 256], U8, name="w1", align_bytes=64)
        w1s = keep.tile([P, 4, 128], U8, name="w1s", align_bytes=64)
        w2 = keep.tile([P, NB, 1024], U8, name="w2", align_bytes=64)
        w2s = keep.tile([P, NB, 512], U8, name="w2s", align_bytes=64)
        w3 = keep.tile([P, 1024], U8, name="w3", align_bytes=64)
        w3s = keep.tile([P, 512], U8, name="w3s", align_bytes=64)
        ident = keep.tile([P, P], F32, name="ident", align_bytes=64)
        s1 = keep.tile([P, 4], BF16, name="s1")
        s1f = keep.tile([P, 4], F32, name="s1f")
        s2 = keep.tile([P, FR, C], BF16, name="s2", align_bytes=64)
        sp = keep.tile([P, FR, 4], BF16, name="sp")
        gate = keep.tile([P, FR, 4], F32, name="gate")
        warm = keep.tile([P, 1], F32, name="warm")
        xg = [keep.tile([P, C, 4], BF16, name=f"xg{f}", align_bytes=64) for f in range(FR)]
        xc = [keep.tile([P, C], U32, name=f"xc{f}", align_bytes=64) for f in range(FR)]
        xs = [keep.tile([P, C], U8, name=f"xs{f}", align_bytes=64) for f in range(FR)]

        with tc.manual_schedule():
            nc.vector.memset(w1s_raw[:].bitcast(I32), 0)
            nc.vector.memset(warm[:], 0.0)
            nc.vector.memset(w2s[:].rearrange("p b n -> p (b n)").bitcast(I32), 0)
            nc.vector.memset(w3s[:].bitcast(I32), 0)
            for q in range(4):
                nc.scalar.dma_start(
                    out=w1s_raw[32 * q : 32 * q + 4, :].bitcast(I32),
                    in_=w1_scales[0, 4 * q : 4 * q + 4, :].bitcast(I32),
                )
            nc.scalar.dma_start(out=s1[:], in_=skip1.rearrange("(p j) -> p j", j=4))
            nc.scalar.dma_start(out=sp[:], in_=speed.rearrange("f (p j) -> p f j", j=4))
            nc.scalar.activation(out=warm[:], in_=warm[:], func=ACT.Tanh)
            make_identity(nc, ident[:])
            xr = []
            for f in range(FR):
                t = raws.tile([P, 4, C], BF16, name="xraw", align_bytes=64)
                nc.sync.dma_start(out=t[:], in_=x[f].rearrange("(p j) c -> p j c", j=4))
                xr.append(t)
                if f == 0:
                    nc.sync.dma_start(out=w1_raw[:].bitcast(I32), in_=w1_words[0].bitcast(I32))
            nc.sync.dma_start(
                out=s2[:].rearrange("p f c -> p (f c)"),
                in_=skip2.rearrange("f c -> (f c)").partition_broadcast(P),
            )
            nc.sync.dma_start(
                out=w2[:].bitcast(I32), in_=w2_words.rearrange("g p n -> p g n").bitcast(I32)
            )
            for q in range(4):
                nc.sync.dma_start(
                    out=w2s[32 * q : 32 * q + 4, :, :].bitcast(I32),
                    in_=w2_scales[:, 4 * q : 4 * q + 4, :].rearrange("g r n -> r g n").bitcast(I32),
                )
            nc.sync.dma_start(out=w3[:].bitcast(I32), in_=w3_words[0].bitcast(I32))
            for q in range(4):
                nc.sync.dma_start(
                    out=w3s[32 * q : 32 * q + 4, :].bitcast(I32),
                    in_=w3_scales[0, 4 * q : 4 * q + 4, :].bitcast(I32),
                )

            def group_w1(j0, j1):
                nc.vector.tensor_copy(
                    out=w1s[:, j0:j1], in_=w1s_raw[:].rearrange("p (m j) -> p j m", j=4)[:, j0:j1]
                )
                nc.vector.tensor_copy(
                    out=w1[:].rearrange("p j (m e) -> p j m e", e=2)[:, j0:j1],
                    in_=w1_raw[:].rearrange("p (m j e) -> p j m e", j=4, e=2)[:, j0:j1],
                )

            def interleave(f, eng, t0, t1):
                a0, a1 = 32 * t0, 32 * t1
                dst = xg[f][:].rearrange("p (t a) j -> p a j t", t=4)[:, a0:a1]
                src = xr[f][:].rearrange("p j (a t) -> p a j t", t=4)[:, a0:a1]
                if eng == "v":
                    nc.vector.tensor_copy(out=dst, in_=src)
                elif eng == "g":
                    nc.gpsimd.tensor_scalar(
                        out=dst, in0=src, scalar1=1.0, scalar2=0.0, op0=ALU.mult, op1=ALU.add
                    )
                else:
                    nc.scalar.copy(out=dst, in_=src)

            def quant_x(f):
                nc.vector.quantize_mx(
                    out=xc[f][:].bitcast(E4M3),
                    scales=xs[f][:],
                    in_=xg[f][:].rearrange("p c j -> p (c j)"),
                )

            state = {}

            def stage1_mm(k, f):
                ps = psv.tile([P, C], F32, name="pv")
                nc.tensor.matmul_mx(
                    out=ps[:],
                    lhsT=w1[:, k, :].bitcast(E2M1),
                    lhsT_scale=w1s[:, k, :],
                    rhs=xc[f][:].bitcast(E4M3),
                    rhs_scale=xs[f][:],
                    start=True,
                    stop=True,
                )
                state[("p1", k, f)] = ps

            def stage1_exit(k, f):
                if ("y", k) not in state:
                    ytile = ys3.tile([P, 32, P], F32, name="y", align_bytes=64)
                    state[("y", k)] = ytile
                y = state[("y", k)]
                nc.vector.scalar_tensor_tensor(
                    out=y[:, :, 16 * f : 16 * f + 16],
                    in0=xg[f][:, :, k].rearrange("p (a q) -> p a q", q=16),
                    scalar=s1f[:, k : k + 1],
                    in1=state[("p1", k, f)][:].rearrange("p (a q) -> p a q", q=16),
                    op0=ALU.mult,
                    op1=ALU.add,
                )

            def skip_y(k, b, eng):
                if ("y2", k, b // 2) not in state:
                    y2 = y2s.tile([P, 2, C], F32, name="y2", align_bytes=64)
                    state[("y2", k, b // 2)] = y2
                y = state[("y", k)]
                eng.tensor_tensor(
                    out=state[("y2", k, b // 2)][:, b % 2].rearrange("p (f q t) -> p f q t", f=FR, t=4),
                    in0=y[:].rearrange("p (t b) (f q) -> p b f q t", t=4, q=16)[:, b],
                    in1=s2[:, :, 64 * b : 64 * b + 64].rearrange("p f (q t) -> p f q t", t=4),
                    op=ALU.mult,
                )

            def y_turn(k, b):
                y = state[("y", k)]
                ps = pss.tile([P, 4, P], F32, name="pt")
                for t in range(4):
                    nc.tensor.transpose(ps[:, t, :], y[:, 8 * t + b, :], ident[:])
                state[("pt", k, b)] = ps

            def y_turn_exit(k, b, eng):
                if ("yT", k) not in state:
                    ytile = once.tile([P, NB, P, 4], BF16, name="yT", align_bytes=64)
                    state[("yT", k)] = ytile
                dst = state[("yT", k)][:, b]
                src = state[("pt", k, b)][:].rearrange("p t n -> p n t")
                if eng == "v":
                    nc.vector.tensor_copy(out=dst, in_=src)
                else:
                    nc.scalar.copy(out=dst, in_=src)

            def quant_y(k, h):
                if ("yc", k) not in state:
                    yc = work.tile([P, NB * P], U32, name="yc", align_bytes=64)
                    ys = work.tile([P, NB * P], U8, name="ys", align_bytes=64)
                    state[("yc", k)] = (yc, ys)
                yc, ys = state[("yc", k)]
                nc.vector.quantize_mx(
                    out=yc[:, 512 * h : 512 * h + 512].bitcast(E4M3),
                    scales=ys[:, 512 * h : 512 * h + 512],
                    in_=state[("yT", k)][:, 4 * h : 4 * h + 4].rearrange("p b n t -> p (b n t)"),
                )

            def stage2_mm(k, m, h):
                yc, ys = state[("yc", k)]
                ps = psv.tile([P, 2, C // 2], F32, name="pv")
                for i in range(2):
                    b = 2 * m + i
                    nc.tensor.matmul_mx(
                        out=ps[:, i, :],
                        lhsT=yc[:, P * b : P * b + P].bitcast(E4M3),
                        lhsT_scale=ys[:, P * b : P * b + P],
                        rhs=w2[:, b, 512 * h : 512 * h + 512].bitcast(E2M1),
                        rhs_scale=w2s[:, b, 256 * h : 256 * h + 256],
                        start=True,
                        stop=True,
                    )
                state[("p2", k, m, h)] = ps

            def stage2_exit(k, m, h):
                if ("z", k) not in state:
                    ztile = once.tile([P, FR, NB, 64], BF16, name="z", align_bytes=64)
                    state[("z", k)] = ztile
                nc.vector.tensor_tensor(
                    out=state[("z", k)][:, 4 * h : 4 * h + 4, 2 * m : 2 * m + 2, :].rearrange("p f b d -> p b f d"),
                    in0=state[("p2", k, m, h)][:].rearrange("p b (f d) -> p b f d", f=4),
                    in1=state[("y2", k, m)][:, :, 256 * h : 256 * h + 256].rearrange("p b (f d) -> p b f d", f=4),
                    op=ALU.add,
                )

            def z_turn(k, g):
                zw = state[("z", k)][:].rearrange("p f b d -> p (f b d)").bitcast(F32)
                ps = pss.tile([P, 4, P], F32, name="pt")
                for i in range(4):
                    f, u = 2 * g + i // 2, i % 2
                    nc.tensor.transpose(
                        ps[:, i, :], zw[:, 256 * f + u : 256 * f + 256 : 2], ident[:]
                    )
                state[("pz", k, g)] = ps

            def z_turn_exit(k, g, eng):
                if ("zT", k) not in state:
                    ztile = once.tile([P, FR, P, 4], BF16, name="zT", align_bytes=64)
                    state[("zT", k)] = ztile
                words = state[("zT", k)][:].rearrange("p f n t -> p (f n t)").bitcast(F32)
                dst = words[:, 512 * g : 512 * g + 512].rearrange("p (f n u) -> p f n u", f=2, u=2)
                src = state[("pz", k, g)][:].rearrange("p (f u) n -> p f n u", u=2)
                if eng == "v":
                    nc.vector.tensor_copy(out=dst, in_=src)
                else:
                    nc.scalar.copy(out=dst, in_=src)

            def quant_z(k, h):
                if ("zc", k) not in state:
                    zc = work.tile([P, FR * P], U32, name="zc", align_bytes=64)
                    zs = work.tile([P, FR * P], U8, name="zs", align_bytes=64)
                    state[("zc", k)] = (zc, zs)
                zc, zs = state[("zc", k)]
                nc.vector.quantize_mx(
                    out=zc[:, 512 * h : 512 * h + 512].bitcast(E4M3),
                    scales=zs[:, 512 * h : 512 * h + 512],
                    in_=state[("zT", k)][:, 4 * h : 4 * h + 4].rearrange("p f n t -> p (f n t)"),
                )

            def stage3_mm(k, f):
                zc, zs = state[("zc", k)]
                ps = pss.tile([P, C], F32, name="pt")
                nc.tensor.matmul_mx(
                    out=ps[:],
                    lhsT=zc[:, P * f : P * f + P].bitcast(E4M3),
                    lhsT_scale=zs[:, P * f : P * f + P],
                    rhs=w3[:].bitcast(E2M1),
                    rhs_scale=w3s[:],
                    start=True,
                    stop=True,
                )
                state[("p3", k, f)] = ps

            def stage3_exit(k, f, eng):
                ps = state[("p3", k, f)]
                o = outs.tile([P, C], F32, name="o", align_bytes=64)
                if eng == "s":
                    nc.scalar.activation(
                        out=o[:], in_=ps[:], func=ACT.Copy, scale=gate[:, f, k : k + 1]
                    )
                else:
                    nc.vector.tensor_scalar(
                        out=o[:], in0=ps[:], scalar1=gate[:, f, k : k + 1], scalar2=None, op0=ALU.mult
                    )
                nc.sync.dma_start(
                    out=out[f].rearrange("(p j) o -> p j o", j=4)[:, k, :], in_=o[:]
                )

            def gate_tanh():
                nc.scalar.activation(
                    out=gate[:].rearrange("p f j -> p (f j)"),
                    in_=sp[:].rearrange("p f j -> p (f j)"),
                    func=ACT.Tanh,
                )

            interleave(0, "v", 0, 1)
            interleave(0, "s", 1, 3)
            interleave(0, "g", 3, 4)
            group_w1(0, 1); nc.vector.tensor_copy(out=s1f[:], in_=s1[:])
            interleave(1, "v", 0, 1)
            interleave(1, "s", 1, 4)
            group_w1(1, 4)
            quant_x(0)
            stage1_mm(0, 0)
            stage1_mm(1, 0)
            interleave(2, "v", 0, 1)
            interleave(2, "s", 1, 3)
            interleave(2, "g", 3, 4)
            quant_x(1)
            stage1_mm(0, 1)
            stage1_mm(1, 1)
            stage1_exit(0, 0)
            stage1_exit(1, 0)
            interleave(3, "s", 0, 3)
            interleave(3, "g", 3, 4)
            quant_x(2); gate_tanh()
            stage1_mm(0, 2)
            stage1_mm(1, 2)
            stage1_exit(0, 1)
            stage1_exit(1, 1)
            interleave(4, "s", 0, 4)
            quant_x(3)
            stage1_mm(0, 3)
            stage1_mm(1, 3)
            stage1_exit(0, 2)
            stage1_exit(1, 2)
            interleave(5, "s", 0, 3)
            interleave(5, "g", 3, 4)
            quant_x(4)
            stage1_mm(0, 4)
            stage1_mm(1, 4)
            stage1_exit(0, 3)
            stage1_exit(1, 3)
            interleave(6, "s", 0, 3)
            interleave(6, "g", 3, 4)
            quant_x(5)
            stage1_mm(0, 5)
            stage1_mm(1, 5)
            stage1_exit(0, 4)
            stage1_exit(1, 4)
            interleave(7, "s", 0, 3)
            interleave(7, "g", 3, 4)
            quant_x(6)
            stage1_mm(0, 6)
            stage1_mm(1, 6)
            stage1_exit(0, 5)
            stage1_exit(1, 5)
            quant_x(7)
            stage1_mm(0, 7)
            stage1_mm(1, 7)
            stage1_exit(0, 6)
            stage1_exit(1, 6)
            stage1_exit(0, 7)
            stage1_exit(1, 7)
            skip_y(0, 0, nc.vector)
            stage1_mm(2, 3)
            stage1_mm(2, 0)
            stage1_exit(2, 3)
            y_turn(0, 3)
            y_turn(0, 4)
            y_turn_exit(0, 3, "s")
            skip_y(0, 6, nc.gpsimd)
            skip_y(0, 1, nc.gpsimd)
            stage1_mm(2, 2)
            y_turn_exit(0, 4, "s")
            y_turn(0, 0)
            stage1_mm(2, 4)
            stage1_exit(2, 2)
            y_turn(0, 2)
            stage1_exit(2, 0)
            y_turn_exit(0, 0, "s")
            y_turn(0, 1)
            y_turn_exit(0, 2, "v")
            skip_y(0, 5, nc.gpsimd)
            stage1_mm(2, 5)
            stage1_exit(2, 4)
            y_turn_exit(0, 1, "s")
            y_turn(0, 6)
            stage1_mm(2, 1)
            stage1_exit(2, 5)
            y_turn_exit(0, 6, "s")
            skip_y(0, 7, nc.gpsimd)
            stage1_exit(2, 1)
            y_turn(0, 7)
            skip_y(0, 2, nc.vector)
            y_turn(0, 5)
            y_turn_exit(0, 7, "s")
            stage1_mm(2, 7)
            quant_y(0, 0)
            y_turn_exit(0, 5, "s")
            stage1_mm(2, 6)
            stage2_mm(0, 0, 0)
            stage1_exit(2, 7)
            stage1_exit(2, 6)
            skip_y(0, 3, nc.gpsimd)
            stage2_mm(0, 1, 0)
            quant_y(0, 1)
            stage2_exit(0, 1, 0)
            stage2_mm(0, 3, 0)
            stage2_exit(0, 0, 0)
            stage2_mm(0, 2, 0)
            stage2_exit(0, 3, 0)
            skip_y(0, 4, nc.gpsimd)
            stage2_mm(0, 1, 1)
            stage2_mm(0, 3, 1)
            stage2_mm(0, 0, 1)
            stage2_exit(0, 2, 0)
            stage2_exit(0, 1, 1)
            stage2_exit(0, 3, 1)
            stage2_mm(0, 2, 1)
            stage2_exit(0, 2, 1)
            z_turn(0, 1)
            stage2_exit(0, 0, 1)
            skip_y(1, 0, nc.gpsimd)
            stage1_mm(3, 3)
            stage1_mm(3, 0)
            z_turn_exit(0, 1, "s")
            z_turn(0, 0)
            stage1_exit(3, 3)
            y_turn(1, 3)
            y_turn(1, 4)
            z_turn_exit(0, 0, "v")
            y_turn_exit(1, 3, "s")
            skip_y(1, 6, nc.gpsimd)
            skip_y(1, 1, nc.vector)
            z_turn(0, 2)
            stage1_mm(3, 2)
            y_turn_exit(1, 4, "s")
            quant_z(0, 0)
            z_turn(0, 3)
            y_turn(1, 0)
            stage1_mm(3, 4)
            stage1_exit(3, 2)
            y_turn(1, 2)
            z_turn_exit(0, 2, "s")
            stage1_exit(3, 0)
            z_turn_exit(0, 3, "s")
            y_turn_exit(1, 0, "s")
            y_turn(1, 1)
            y_turn_exit(1, 2, "s")
            skip_y(1, 5, nc.gpsimd)
            stage1_mm(3, 5)
            quant_z(0, 1)
            stage1_exit(3, 4)
            y_turn_exit(1, 1, "s")
            y_turn(1, 6)
            stage1_mm(3, 1)
            stage1_exit(3, 5)
            y_turn_exit(1, 6, "v")
            skip_y(1, 7, nc.gpsimd)
            stage1_exit(3, 1)
            y_turn(1, 7)
            skip_y(1, 2, nc.gpsimd)
            y_turn(1, 5)
            y_turn_exit(1, 7, "s")
            stage1_mm(3, 7)
            stage3_mm(0, 0)
            quant_y(1, 0)
            stage3_mm(0, 1)
            y_turn_exit(1, 5, "s")
            stage3_mm(0, 5)
            stage3_exit(0, 0, "s")
            stage1_mm(3, 6)
            stage3_exit(0, 1, "s")
            stage2_mm(1, 0, 0)
            stage1_exit(3, 7)
            stage1_exit(3, 6)
            skip_y(1, 3, nc.gpsimd)
            stage2_mm(1, 1, 0)
            stage3_exit(0, 5, "s")
            stage3_mm(0, 6)
            stage3_mm(0, 3)
            quant_y(1, 1)
            stage2_exit(1, 1, 0)
            stage2_mm(1, 3, 0)
            stage3_mm(0, 7)
            stage2_exit(1, 0, 0)
            stage2_mm(1, 2, 0)
            stage2_exit(1, 3, 0)
            stage3_exit(0, 6, "s")
            skip_y(1, 4, nc.gpsimd)
            stage3_exit(0, 3, "s")
            stage3_exit(0, 7, "s")
            stage3_mm(0, 4)
            stage2_mm(1, 1, 1)
            stage3_exit(0, 4, "s")
            stage2_mm(1, 3, 1)
            stage2_mm(1, 0, 1)
            stage3_mm(0, 2)
            stage2_exit(1, 2, 0)
            stage2_exit(1, 1, 1)
            stage2_exit(1, 3, 1)
            stage2_mm(1, 2, 1)
            stage2_exit(1, 2, 1)
            z_turn(1, 1)
            stage2_exit(1, 0, 1)
            skip_y(2, 0, nc.gpsimd)
            stage3_exit(0, 2, "s")
            z_turn_exit(1, 1, "s")
            z_turn(1, 0)
            y_turn(2, 3)
            y_turn(2, 4)
            z_turn_exit(1, 0, "s")
            y_turn_exit(2, 3, "s")
            skip_y(2, 6, nc.gpsimd)
            skip_y(2, 1, nc.gpsimd)
            z_turn(1, 2)
            y_turn_exit(2, 4, "v")
            quant_z(1, 0)
            z_turn(1, 3)
            y_turn(2, 0)
            y_turn(2, 2)
            z_turn_exit(1, 2, "s")
            z_turn_exit(1, 3, "s")
            y_turn_exit(2, 0, "v")
            y_turn(2, 1)
            y_turn_exit(2, 2, "v")
            skip_y(2, 5, nc.gpsimd)
            quant_z(1, 1)
            y_turn_exit(2, 1, "v")
            y_turn(2, 6)
            y_turn_exit(2, 6, "s")
            skip_y(2, 7, nc.gpsimd)
            y_turn(2, 7)
            skip_y(2, 2, nc.vector)
            y_turn(2, 5)
            y_turn_exit(2, 7, "s")
            stage3_mm(1, 0)
            quant_y(2, 0)
            stage3_mm(1, 1)
            y_turn_exit(2, 5, "v")
            stage3_mm(1, 5)
            stage3_exit(1, 0, "v")
            stage3_exit(1, 1, "s")
            stage2_mm(2, 0, 0)
            skip_y(2, 3, nc.gpsimd)
            stage2_mm(2, 1, 0)
            stage3_exit(1, 5, "s")
            stage3_mm(1, 6)
            stage3_mm(1, 3)
            quant_y(2, 1)
            stage2_exit(2, 1, 0)
            stage2_mm(2, 3, 0)
            stage3_mm(1, 7)
            stage2_exit(2, 0, 0)
            stage2_mm(2, 2, 0)
            stage2_exit(2, 3, 0)
            stage3_exit(1, 6, "s")
            skip_y(2, 4, nc.gpsimd)
            stage3_exit(1, 3, "s")
            stage3_exit(1, 7, "s")
            stage3_mm(1, 4)
            stage2_mm(2, 1, 1)
            stage3_exit(1, 4, "s")
            stage2_mm(2, 3, 1)
            stage2_mm(2, 0, 1)
            stage3_mm(1, 2)
            stage2_exit(2, 2, 0)
            stage2_exit(2, 1, 1)
            stage2_exit(2, 3, 1)
            stage2_mm(2, 2, 1)
            stage2_exit(2, 2, 1)
            z_turn(2, 1)
            stage2_exit(2, 0, 1)
            skip_y(3, 0, nc.gpsimd)
            stage3_exit(1, 2, "s")
            z_turn_exit(2, 1, "s")
            z_turn(2, 0)
            y_turn(3, 3)
            y_turn(3, 4)
            z_turn_exit(2, 0, "s")
            y_turn_exit(3, 3, "v")
            skip_y(3, 6, nc.gpsimd)
            skip_y(3, 1, nc.gpsimd)
            z_turn(2, 2)
            y_turn_exit(3, 4, "v")
            quant_z(2, 0)
            z_turn(2, 3)
            y_turn(3, 0)
            y_turn(3, 2)
            z_turn_exit(2, 2, "s")
            z_turn_exit(2, 3, "v")
            y_turn_exit(3, 0, "s")
            y_turn(3, 1)
            y_turn_exit(3, 2, "s")
            skip_y(3, 5, nc.gpsimd)
            quant_z(2, 1)
            y_turn_exit(3, 1, "s")
            y_turn(3, 6)
            y_turn_exit(3, 6, "s")
            skip_y(3, 7, nc.vector)
            y_turn(3, 7)
            skip_y(3, 2, nc.vector)
            y_turn(3, 5)
            y_turn_exit(3, 7, "s")
            stage3_mm(2, 0)
            quant_y(3, 0)
            stage3_mm(2, 1)
            y_turn_exit(3, 5, "s")
            stage3_mm(2, 5)
            stage3_exit(2, 0, "s")
            stage3_exit(2, 1, "s")
            stage2_mm(3, 0, 0)
            skip_y(3, 3, nc.gpsimd)
            stage2_mm(3, 1, 0)
            stage3_exit(2, 5, "s")
            stage3_mm(2, 6)
            stage3_mm(2, 3)
            quant_y(3, 1)
            stage2_exit(3, 1, 0)
            stage2_mm(3, 3, 0)
            stage3_mm(2, 7)
            stage2_exit(3, 0, 0)
            stage2_mm(3, 2, 0)
            stage2_exit(3, 3, 0)
            stage3_exit(2, 6, "s")
            skip_y(3, 4, nc.gpsimd)
            stage3_exit(2, 3, "s")
            stage3_exit(2, 7, "s")
            stage3_mm(2, 4)
            stage2_mm(3, 1, 1)
            stage3_exit(2, 4, "s")
            stage2_mm(3, 3, 1)
            stage2_mm(3, 0, 1)
            stage3_mm(2, 2)
            stage2_exit(3, 2, 0)
            stage2_exit(3, 1, 1)
            stage2_exit(3, 3, 1)
            stage2_mm(3, 2, 1)
            stage2_exit(3, 2, 1)
            z_turn(3, 1)
            stage2_exit(3, 0, 1)
            stage3_exit(2, 2, "s")
            z_turn_exit(3, 1, "s")
            z_turn(3, 0)
            z_turn_exit(3, 0, "s")
            z_turn(3, 2)
            quant_z(3, 0)
            z_turn(3, 3)
            z_turn_exit(3, 2, "v")
            z_turn_exit(3, 3, "s")
            quant_z(3, 1)
            stage3_mm(3, 0)
            stage3_mm(3, 1)
            stage3_mm(3, 5)
            stage3_exit(3, 0, "s")
            stage3_exit(3, 1, "s")
            stage3_exit(3, 5, "v")
            stage3_mm(3, 6)
            stage3_mm(3, 3)
            stage3_mm(3, 7)
            stage3_exit(3, 6, "s")
            stage3_exit(3, 3, "v")
            stage3_exit(3, 7, "s")
            stage3_mm(3, 4)
            stage3_exit(3, 4, "s")
            stage3_mm(3, 2)
            stage3_exit(3, 2, "v")
